import numpy as np
import ml_dtypes


def mxq(x, axis, fmt="e4m3"):
    dtype, down = {"e4m3": (ml_dtypes.float8_e4m3fn, 7), "e5m2": (ml_dtypes.float8_e5m2, 14)}[fmt]
    v = np.moveaxis(np.asarray(x, np.float32).astype(ml_dtypes.bfloat16).astype(np.float64), axis, -1)
    blocks = v.reshape(v.shape[:-1] + (-1, 32))
    amax = np.abs(blocks).max(-1, keepdims=True)
    byte = np.maximum(np.where(amax > 0, np.frexp(amax)[1] - 1 + 127, 0) - down, 1)
    scale = np.exp2(byte - 127.0)
    codes = (blocks / scale).astype(np.float32).astype(dtype).astype(np.float64)
    return np.moveaxis((codes * scale).reshape(v.shape), -1, axis)


WIDE = False


def mx_kscale(k):
    if not WIDE:
        return np.ones(k)
    levels = np.array([30, -30])
    if k % 512:
        return np.exp2(np.random.permutation(np.resize(levels, k // 32))).repeat(32)
    a = np.empty((k // 512, 16))
    for p in range(k // 512):
        a[p, :8] = np.random.permutation(np.resize(levels, 8))
        for g in range(8):
            far = levels[np.abs(levels - a[p, g]) >= 10]
            a[p, g + 8] = far[np.random.randint(len(far))]
    return np.exp2(a.ravel()).repeat(32)


def f64(x):
    return np.asarray(x).astype(np.float64)


def striped(idx):
    return np.tile(np.asarray(idx).reshape(-1, 16).T, (8, 1)).astype(np.uint16)


def unstriped(offs):
    return offs[:16].T.reshape(-1).astype(np.int64)


E2M1 = np.array([0.0, 0.5, 1.0, 1.5, 2.0, 3.0, 4.0, 6.0, -0.0, -0.5, -1.0, -1.5, -2.0, -3.0, -4.0, -6.0])


def pack_weight(w, fmt):
    k, n = w.shape
    w = f64(np.asarray(w, np.float32).astype(ml_dtypes.bfloat16)).reshape(k // 32, 32, n)
    amax = np.abs(w).max(1)
    if fmt in ("e4m3", "e5m2"):
        byte = np.frexp(amax)[1] - 1 + 127 - (7 if fmt == "e4m3" else 14)
    else:
        mant, ex = np.frexp(amax / 6.0)
        byte = np.where(mant > 0.5, ex, ex - 1) + 127
    byte = np.clip(np.where(amax > 0, byte, 1), 1, 254)
    scaled = (w * np.exp2(127.0 - byte)[:, None, :]).reshape(k, n).astype(np.float32)
    by_word = np.ascontiguousarray(scaled.reshape(k // 512, 128, 4, n).transpose(0, 1, 3, 2))
    if fmt in ("e4m3", "e5m2"):
        words = by_word.astype(ml_dtypes.float8_e4m3fn if fmt == "e4m3" else ml_dtypes.float8_e5m2).view(np.uint8)
    else:
        c = by_word.astype(ml_dtypes.float4_e2m1fn).view(np.uint8) & 0xF
        words = (c[..., 0::2] | (c[..., 1::2] << 4)).reshape(k // 512, 128, 2 * n)
    return np.ascontiguousarray(words), np.ascontiguousarray(byte.astype(np.uint8).reshape(k // 512, 16, n))


def unpack_weight(words, scales, fmt):
    g, _, n = scales.shape
    words = np.ascontiguousarray(words).reshape(g, 128, n, -1)
    if fmt in ("e4m3", "e5m2"):
        vals = words.view(ml_dtypes.float8_e4m3fn if fmt == "e4m3" else ml_dtypes.float8_e5m2).astype(np.float64)
    else:
        nib = np.empty((g, 128, n, 4), np.uint8)
        nib[..., 0::2] = words & 0xF
        nib[..., 1::2] = words >> 4
        vals = E2M1[nib]
    vals = vals * np.repeat(np.exp2(scales.astype(np.float64) - 127.0), 8, axis=1)[..., None]
    return vals.transpose(0, 1, 3, 2).reshape(g * 512, n)


def bf(x):
    return np.asarray(x, np.float32).astype(ml_dtypes.bfloat16)


def planes(Y):
    r, m = Y.shape
    b = f64(bf(Y)).reshape(r // 32, 32, m)
    amax = np.abs(b).max(1)
    byte = np.clip(np.where(amax > 0, np.frexp(amax)[1] - 1 + 127 - 7, 1), 1, 254)
    codes = (b * np.exp2(127.0 - byte)[:, None, :]).reshape(r, m).astype(np.float32).astype(ml_dtypes.float8_e4m3fn).view(np.uint8)
    words = codes.reshape(r // 512, 128, 4, m).transpose(0, 1, 3, 2)
    return np.ascontiguousarray(words), np.ascontiguousarray(byte.astype(np.uint8).reshape(r // 512, 16, m))


K, T, J, R, G, N, Z = 512, 512, 256, 512, 64, 512, 512


def setup_inputs():
    n = np.random.standard_normal
    idx = np.random.permutation(T)[:J]
    idx2 = np.random.permutation(T)[:J]
    idx3 = np.random.permutation(Z)[:J]
    fk = mx_kscale(K)
    fr = mx_kscale(R)
    wp = pack_weight(n((K, R)) * 1 / np.sqrt(K) * fk[:, None], "e5m2")
    wbp = pack_weight(n((R, N)) * 1 / np.sqrt(R) / fr[:, None], "e4m3")
    return {
        "xf": (n((K, T))).astype(np.float32),
        "fk": (np.random.uniform(0.5, 2.0, (K, 1)) / fk[:, None]).astype(np.float32),
        "w_words": wp[0],
        "w_scales": wp[1],
        "us": (np.random.uniform(0.5, 1.5, (1, R)) * fr).astype(np.float32),
        "wb_words": wbp[0],
        "wb_scales": wbp[1],
        "tz": (n((N, Z))).astype(np.float32),
        "offs": striped(idx),
        "offs2": striped(idx2),
        "offs3": striped(idx3),
    }


def reference(xf, fk, w_words, w_scales, us, wb_words, wb_scales, tz, offs, offs2, offs3):
    idx = unstriped(offs)
    idx2 = unstriped(offs2)
    idx3 = unstriped(offs3)
    wu = unpack_weight(w_words, w_scales, "e5m2")
    wbu = unpack_weight(wb_words, wb_scales, "e4m3")
    u = (f64(xf)[:, idx] - f64(xf)[:, idx2]) * f64(fk)
    uq = mxq(u, 0, "e5m2")
    a = uq.T @ wu
    m1 = a.reshape(J, G, R // G).max(axis=2)
    m2 = np.repeat(m1, R // G, axis=1)
    hr = np.maximum(a - 0.5 * m2, 0.0) * f64(us)
    hid = hr.T
    hidq = mxq(hid, 0, "e5m2")
    p = wbu.T @ hidq
    y = p * f64(tz)[:, idx3]
    words, scales = planes(y)
    return y, words, scales

@@ -1,0 +1,227 @@
+from contextlib import ExitStack
+
+import concourse.mybir as mybir
+from concourse.masks import make_identity
+
+K, T, J, R, N, Z = 512, 512, 256, 512, 512, 512
+FLOPS = 2 * K * J * R + 2 * R * N * J
+
+F32 = mybir.dt.float32
+BF16 = mybir.dt.bfloat16
+I32 = mybir.dt.int32
+U32 = mybir.dt.uint32
+U16 = mybir.dt.uint16
+U8 = mybir.dt.uint8
+E5M2 = mybir.dt.float8_e5m2_x4
+E4M3 = mybir.dt.float8_e4m3fn_x4
+ALU = mybir.AluOpType
+COPY = mybir.ActivationFunctionType.Copy
+
+P = 128
+PACK = 4
+HALVES = 2
+S = J // HALVES
+LIST_COLS = S // 16
+BUNDLE = 8
+R_BANK = R // 2
+
+
+def tile_list_rows_pickgaps_grouppeaks_timeslook_pl_kernel(
+    tc, xf, fk, w_words, w_scales, us, wb_words, wb_scales, tz, offs, offs2, offs3, out_0, out_1, out_2
+):
+    nc = tc.nc
+    with ExitStack() as ctx:
+        sb = ctx.enter_context(tc.tile_pool(name="sb", bufs=1))
+        ps = ctx.enter_context(tc.psum_pool(name="ps", bufs=1))
+
+        def tiles(pool, name, count, shape, dtype):
+            return [
+                pool.tile(shape, dtype, name="%s%d" % (name, i), tag="%s%d" % (name, i), align_bytes=64)
+                for i in range(count)
+            ]
+
+        def banks(name, count, shape):
+            return [ps.tile(shape, F32, name="%s%d" % (name, i), tag="%s%d" % (name, i)) for i in range(count)]
+
+        def load_scales(plane, scales):
+            for q in range(4):
+                nc.sync.dma_start(
+                    out=plane[32 * q : 32 * q + 4, :].bitcast(I32), in_=scales[0, 4 * q : 4 * q + 4, :].bitcast(I32)
+                )
+
+        def load_words(words, dram):
+            nc.sync.dma_start(out=words[:].bitcast(I32), in_=dram[0].rearrange("p n t -> p (n t)").bitcast(I32))
+
+        def interleave(copy, grouped, planes):
+            copy(
+                out=grouped.rearrange("p (c i) t -> p c t i", i=4),
+                in_=planes.rearrange("p t (c i) -> p c t i", i=4),
+            )
+
+        def quantize(codes, scales, grouped, fmt):
+            nc.vector.quantize_mx(out=codes.bitcast(fmt), scales=scales, in_=grouped.rearrange("p j t -> p (j t)"))
+
+        list1 = sb.tile([P, J // 16], U16, name="list1")
+        list2 = sb.tile([P, J // 16], U16, name="list2")
+        list3 = sb.tile([P, J // 16], U16, name="list3")
+        x = tiles(sb, "x", PACK, [P, T], F32)
+        table = tiles(sb, "table", PACK, [P, Z], F32)
+        fk_sb = sb.tile([P, PACK], F32, name="fk_sb")
+        us_sb = sb.tile([P, PACK], F32, name="us_sb")
+        w_codes = sb.tile([P, R], U32, name="w_codes", align_bytes=64)
+        w_plane = sb.tile([P, R], U8, name="w_plane", align_bytes=64)
+        wb_raw = sb.tile([P, N], U32, name="wb_raw", align_bytes=64)
+        wb_raw_plane = sb.tile([P, N], U8, name="wb_raw_plane", align_bytes=64)
+        ident = sb.tile([P, P], F32, name="ident")
+
+        nc.vector.memset(w_plane[:].bitcast(I32), 0)
+        nc.vector.memset(wb_raw_plane[:].bitcast(I32), 0)
+        make_identity(nc, ident[:])
+
+        x_rows = xf.rearrange("(p t) c -> p t c", t=PACK)
+        tz_rows = tz.rearrange("(p t) c -> p t c", t=PACK)
+        nc.sync.dma_start(out=list2[:], in_=offs2)
+        nc.sync.dma_start(out=x[0][:], in_=x_rows[:, 0, :])
+        nc.sync.dma_start(out=list1[:], in_=offs)
+        for t in range(1, PACK):
+            nc.sync.dma_start(out=x[t][:], in_=x_rows[:, t, :])
+        nc.sync.dma_start(out=fk_sb[:], in_=fk.rearrange("(p t) o -> p (t o)", t=PACK))
+        load_scales(w_plane, w_scales)
+        load_words(w_codes, w_words)
+        load_scales(wb_raw_plane, wb_scales)
+        load_words(wb_raw, wb_words)
+        nc.sync.dma_start(out=us_sb[:], in_=us.rearrange("o (p t) -> p (o t)", t=PACK))
+        nc.sync.dma_start(out=list3[:], in_=offs3)
+        for t in range(PACK):
+            nc.sync.dma_start(out=table[t][:], in_=tz_rows[:, t, :])
+
+        def part(lst, h):
+            return lst[:, h * LIST_COLS : (h + 1) * LIST_COLS]
+
+        second = tiles(sb, "second", HALVES, [P, PACK, S], F32)
+        gap = tiles(sb, "gap", HALVES, [P, PACK, S], F32)
+        u_planes = tiles(sb, "u_planes", HALVES, [P, PACK, S], BF16)
+        u_grouped = tiles(sb, "u_grouped", HALVES, [P, S, PACK], BF16)
+        u_codes = tiles(sb, "u_codes", HALVES, [P, S], U32)
+        u_scale = tiles(sb, "u_scale", HALVES, [P, S], U8)
+        a_ps = banks("a_ps", 2 * HALVES, [P, R_BANK])
+        a_sb = tiles(sb, "a_sb", HALVES, [P, PACK, P], F32)
+        peak = tiles(sb, "peak", HALVES, [P, R // BUNDLE], F32)
+        d_ps = banks("d_ps", HALVES, [P, PACK, S])
+        h_codes = tiles(sb, "h_codes", HALVES, [P, S], U32)
+        h_scale = tiles(sb, "h_scale", HALVES, [P, S], U8)
+        looked = tiles(sb, "looked", HALVES, [P, PACK, S], F32)
+        y = tiles(sb, "y", HALVES, [P, PACK, S], F32)
+        y_grouped = tiles(sb, "y_grouped", HALVES, [P, S, PACK], BF16)
+        y_codes = sb.tile([P, J], U32, name="y_codes", align_bytes=64)
+        y_scale = sb.tile([P, J], U8, name="y_scale", align_bytes=64)
+
+        for t in range(PACK):
+            for h in range(HALVES):
+                nc.scalar.activation(second[h][:, t, :], x[t][:].indirect(part(list2, h)), COPY)
+                nc.vector.tensor_tensor(
+                    gap[h][:, t, :], x[t][:].indirect(part(list1, h)), second[h][:, t, :], ALU.subtract
+                )
+        for t in range(PACK):
+            for h in range(HALVES):
+                nc.scalar.activation(u_planes[h][:, t, :], gap[h][:, t, :], COPY, scale=fk_sb[:, t : t + 1])
+
+        for h in range(HALVES):
+            interleave(nc.vector.tensor_copy, u_grouped[h][:], u_planes[h][:])
+            quantize(u_codes[h][:], u_scale[h][:], u_grouped[h][:], E5M2)
+            for b in range(2):
+                cols = slice(b * R_BANK, (b + 1) * R_BANK)
+                nc.tensor.matmul_mx(
+                    out=a_ps[2 * h + b][:],
+                    lhsT=u_codes[h][:].bitcast(E5M2),
+                    lhsT_scale=u_scale[h][:],
+                    rhs=w_codes[:, cols].bitcast(E5M2),
+                    rhs_scale=w_plane[:, cols],
+                    start=True,
+                    stop=True,
+                )
+
+        wb_codes = sb.tile([P, PACK, P], U32, name="wb_codes", tag="u_codes1", align_bytes=64)
+        wb_plane = sb.tile([P, PACK, P], U8, name="wb_plane", tag="u_scale1", align_bytes=64)
+        nc.gpsimd.tensor_copy(out=wb_codes[:], in_=wb_raw[:].rearrange("p (m t) -> p t m", t=PACK))
+        nc.gpsimd.tensor_copy(out=wb_plane[:], in_=wb_raw_plane[:].rearrange("p (m t) -> p t m", t=PACK))
+
+        def peaks(h, b):
+            g = R_BANK // BUNDLE
+            nc.vector.tensor_reduce(
+                out=peak[h][:, b * g : (b + 1) * g],
+                in_=a_ps[2 * h + b][:].rearrange("p (g e) -> p g e", e=BUNDLE),
+                axis=mybir.AxisListType.X,
+                op=ALU.max,
+            )
+
+        def above(h, b):
+            g = R_BANK // BUNDLE
+            q = R_BANK // PACK
+            nc.vector.scalar_tensor_tensor(
+                out=a_sb[h][:, :, b * q : (b + 1) * q].rearrange("p t q -> p q t"),
+                in0=peak[h][:, b * g : (b + 1) * g].unsqueeze(2).to_broadcast([P, g, BUNDLE]),
+                scalar=-0.5,
+                in1=a_ps[2 * h + b][:].rearrange("p (g e) -> p g e", e=BUNDLE),
+                op0=ALU.mult,
+                op1=ALU.add,
+            )
+
+        for h in range(HALVES):
+            peaks(h, 0)
+            peaks(h, 1)
+            above(h, 0)
+            above(h, 1)
+            for t in range(PACK):
+                nc.tensor.transpose(d_ps[h][:, t, :], a_sb[h][:, t, :], ident[:])
+
+        p_ps = []
+        for h in range(HALVES):
+            h_grouped = sb.tile([P, S, PACK], BF16, name="h_grouped%d" % h, tag="h_grouped", align_bytes=64)
+            nc.vector.scalar_tensor_tensor(
+                out=h_grouped[:],
+                in0=d_ps[h][:].rearrange("p t j -> p j t"),
+                scalar=0.0,
+                in1=us_sb[:].unsqueeze(1).to_broadcast([P, S, PACK]),
+                op0=ALU.max,
+                op1=ALU.mult,
+            )
+            quantize(h_codes[h][:], h_scale[h][:], h_grouped[:], E5M2)
+            for u in range(2):
+                p_ps.append(ps.tile([P, 2, S], F32, name="p_ps%d" % (2 * h + u), tag="a_ps%d" % (2 * h + u)))
+            for t in range(PACK):
+                nc.tensor.matmul_mx(
+                    out=p_ps[2 * h + t // 2][:, t % 2, :],
+                    lhsT=wb_codes[:, t, :].bitcast(E4M3),
+                    lhsT_scale=wb_plane[:, t, :],
+                    rhs=h_codes[h][:].bitcast(E5M2),
+                    rhs_scale=h_scale[h][:],
+                    start=True,
+                    stop=True,
+                )
+
+        y_rows = out_0.rearrange("(p t) j -> p t j", t=PACK)
+        words = out_1[0].rearrange("p j t -> p (j t)").bitcast(I32)
+        for h in range(HALVES):
+            slots = slice(h * S, (h + 1) * S)
+            for t in range(PACK):
+                nc.scalar.activation(looked[h][:, t, :], table[t][:].indirect(part(list3, h)), COPY)
+            for u in range(2):
+                rows = slice(2 * u, 2 * u + 2)
+                nc.vector.tensor_tensor(y[h][:, rows, :], p_ps[2 * h + u][:], looked[h][:, rows, :], ALU.mult)
+            nc.sync.dma_start(out=y_rows[:, :, slots], in_=y[h][:])
+            if h == 0:
+                nc.scalar.copy(out=y_grouped[h][:], in_=y[h][:].rearrange("p t j -> p j t"))
+                quantize(y_codes[:, slots], y_scale[:, slots], y_grouped[h][:], E4M3)
+            else:
+                quarters = [slice(0, S // 2), slice(S // 2, S)]
+                for c in quarters:
+                    interleave(nc.vector.tensor_copy, y_grouped[h][:, c, :], y[h][:, :, c])
+                for c in quarters:
+                    quantize(y_codes[:, slots][:, c], y_scale[:, slots][:, c], y_grouped[h][:, c, :], E4M3)
+        nc.sync.dma_start(out=words, in_=y_codes[:].bitcast(I32))
+        for q in range(4):
+            queue = nc.scalar if q % 2 == 0 else nc.sync
+            queue.dma_start(
+                out=out_2[0, 4 * q : 4 * q + 4, :].bitcast(I32), in_=y_scale[32 * q : 32 * q + 4, :].bitcast(I32)
+            )

@@ -76,6 +76,9 @@ def tile_list_rows_pickgaps_grouppeaks_timeslook_pl_kernel(
 
         nc.vector.memset(w_plane[:].bitcast(I32), 0)
         nc.vector.memset(wb_raw_plane[:].bitcast(I32), 0)
+        warm = sb.tile([P, 2], F32, name="warm")
+        nc.vector.memset(warm[:, 0:1], 0.0)
+        nc.scalar.activation(warm[:, 1:2], warm[:, 0:1], COPY)
         make_identity(nc, ident[:])
 
         x_rows = xf.rearrange("(p t) c -> p t c", t=PACK)

@@ -103,7 +103,7 @@ def tile_list_rows_pickgaps_grouppeaks_timeslook_pl_kernel(
 
         second = tiles(sb, "second", HALVES, [P, PACK, S], F32)
         gap = tiles(sb, "gap", HALVES, [P, PACK, S], F32)
-        u_planes = tiles(sb, "u_planes", HALVES, [P, PACK, S], BF16)
+        u_planes = tiles(sb, "u_planes", HALVES, [P, PACK - 1, S], BF16)
         u_grouped = tiles(sb, "u_grouped", HALVES, [P, S, PACK], BF16)
         u_codes = tiles(sb, "u_codes", HALVES, [P, S], U32)
         u_scale = tiles(sb, "u_scale", HALVES, [P, S], U8)
@@ -125,12 +125,21 @@ def tile_list_rows_pickgaps_grouppeaks_timeslook_pl_kernel(
                 nc.vector.tensor_tensor(
                     gap[h][:, t, :], x[t][:].indirect(part(list1, h)), second[h][:, t, :], ALU.subtract
                 )
-        for t in range(PACK):
-            for h in range(HALVES):
+        for h in range(HALVES):
+            for t in range(PACK - 1):
                 nc.scalar.activation(u_planes[h][:, t, :], gap[h][:, t, :], COPY, scale=fk_sb[:, t : t + 1])
 
         for h in range(HALVES):
-            interleave(nc.vector.tensor_copy, u_grouped[h][:], u_planes[h][:])
+            nc.vector.tensor_copy(
+                out=u_grouped[h][:, :, 0 : PACK - 1], in_=u_planes[h][:].rearrange("p t j -> p j t")
+            )
+            nc.vector.tensor_scalar(
+                out=u_grouped[h][:, :, PACK - 1],
+                in0=gap[h][:, PACK - 1, :],
+                scalar1=fk_sb[:, PACK - 1 : PACK],
+                scalar2=None,
+                op0=ALU.mult,
+            )
             quantize(u_codes[h][:], u_scale[h][:], u_grouped[h][:], E5M2)
             for b in range(2):
                 cols = slice(b * R_BANK, (b + 1) * R_BANK)
@@ -158,14 +167,15 @@ def tile_list_rows_pickgaps_grouppeaks_timeslook_pl_kernel(
                 op=ALU.max,
             )
 
-        def above(h, b):
+        def above(h, b, ts):
             g = R_BANK // BUNDLE
             q = R_BANK // PACK
+            count = ts.stop - ts.start
             nc.vector.scalar_tensor_tensor(
-                out=a_sb[h][:, :, b * q : (b + 1) * q].rearrange("p t q -> p q t"),
-                in0=peak[h][:, b * g : (b + 1) * g].unsqueeze(2).to_broadcast([P, g, BUNDLE]),
+                out=a_sb[h][:, ts, b * q : (b + 1) * q].rearrange("p t q -> p q t"),
+                in0=peak[h][:, b * g : (b + 1) * g].unsqueeze(2).to_broadcast([P, g, 2 * count]),
                 scalar=-0.5,
-                in1=a_ps[2 * h + b][:].rearrange("p (g e) -> p g e", e=BUNDLE),
+                in1=a_ps[2 * h + b][:].rearrange("p (q t) -> p q t", t=PACK)[:, :, ts],
                 op0=ALU.mult,
                 op1=ALU.add,
             )
@@ -173,10 +183,11 @@ def tile_list_rows_pickgaps_grouppeaks_timeslook_pl_kernel(
         for h in range(HALVES):
             peaks(h, 0)
             peaks(h, 1)
-            above(h, 0)
-            above(h, 1)
-            for t in range(PACK):
-                nc.tensor.transpose(d_ps[h][:, t, :], a_sb[h][:, t, :], ident[:])
+            for ts in [slice(0, PACK)] if h == 0 else [slice(0, 2), slice(2, PACK)]:
+                above(h, 0, ts)
+                above(h, 1, ts)
+                for t in range(ts.start, ts.stop):
+                    nc.tensor.transpose(d_ps[h][:, t, :], a_sb[h][:, t, :], ident[:])
 
         p_ps = []
         for h in range(HALVES):

from contextlib import ExitStack

import concourse.mybir as mybir
from concourse.masks import make_identity

K, T, J, R, N, Z = 512, 512, 256, 512, 512, 512
FLOPS = 2 * K * J * R + 2 * R * N * J

F32 = mybir.dt.float32
BF16 = mybir.dt.bfloat16
I32 = mybir.dt.int32
U32 = mybir.dt.uint32
U16 = mybir.dt.uint16
U8 = mybir.dt.uint8
E5M2 = mybir.dt.float8_e5m2_x4
E4M3 = mybir.dt.float8_e4m3fn_x4
ALU = mybir.AluOpType
COPY = mybir.ActivationFunctionType.Copy

P = 128
PACK = 4
HALVES = 2
S = J // HALVES
LIST_COLS = S // 16
BUNDLE = 8
R_BANK = R // 2


def tile_list_rows_pickgaps_grouppeaks_timeslook_pl_kernel(
    tc, xf, fk, w_words, w_scales, us, wb_words, wb_scales, tz, offs, offs2, offs3, out_0, out_1, out_2
):
    nc = tc.nc
    with ExitStack() as ctx:
        sb = ctx.enter_context(tc.tile_pool(name="sb", bufs=1))
        ps = ctx.enter_context(tc.psum_pool(name="ps", bufs=1))

        def tiles(pool, name, count, shape, dtype):
            return [
                pool.tile(shape, dtype, name="%s%d" % (name, i), tag="%s%d" % (name, i), align_bytes=64)
                for i in range(count)
            ]

        def banks(name, count, shape):
            return [ps.tile(shape, F32, name="%s%d" % (name, i), tag="%s%d" % (name, i)) for i in range(count)]

        def load_scales(plane, scales):
            for q in range(4):
                nc.sync.dma_start(
                    out=plane[32 * q : 32 * q + 4, :].bitcast(I32), in_=scales[0, 4 * q : 4 * q + 4, :].bitcast(I32)
                )

        def load_words(words, dram):
            nc.sync.dma_start(out=words[:].bitcast(I32), in_=dram[0].rearrange("p n t -> p (n t)").bitcast(I32))

        def interleave(copy, grouped, planes):
            copy(
                out=grouped.rearrange("p (c i) t -> p c t i", i=4),
                in_=planes.rearrange("p t (c i) -> p c t i", i=4),
            )

        def quantize(codes, scales, grouped, fmt):
            nc.vector.quantize_mx(out=codes.bitcast(fmt), scales=scales, in_=grouped.rearrange("p j t -> p (j t)"))

        list1 = sb.tile([P, J // 16], U16, name="list1")
        list2 = sb.tile([P, J // 16], U16, name="list2")
        list3 = sb.tile([P, J // 16], U16, name="list3")
        x = tiles(sb, "x", PACK, [P, T], F32)
        table = tiles(sb, "table", PACK, [P, Z], F32)
        fk_sb = sb.tile([P, PACK], F32, name="fk_sb")
        us_sb = sb.tile([P, PACK], F32, name="us_sb")
        w_codes = sb.tile([P, R], U32, name="w_codes", align_bytes=64)
        w_plane = sb.tile([P, R], U8, name="w_plane", align_bytes=64)
        wb_raw = sb.tile([P, N], U32, name="wb_raw", align_bytes=64)
        wb_raw_plane = sb.tile([P, N], U8, name="wb_raw_plane", align_bytes=64)
        ident = sb.tile([P, P], F32, name="ident")

        nc.vector.memset(w_plane[:].bitcast(I32), 0)
        nc.vector.memset(wb_raw_plane[:].bitcast(I32), 0)
        warm = sb.tile([P, 2], F32, name="warm")
        nc.vector.memset(warm[:, 0:1], 0.0)
        nc.scalar.activation(warm[:, 1:2], warm[:, 0:1], COPY)
        make_identity(nc, ident[:])

        x_rows = xf.rearrange("(p t) c -> p t c", t=PACK)
        tz_rows = tz.rearrange("(p t) c -> p t c", t=PACK)
        nc.sync.dma_start(out=list2[:], in_=offs2)
        nc.sync.dma_start(out=x[0][:], in_=x_rows[:, 0, :])
        nc.sync.dma_start(out=list1[:], in_=offs)
        for t in range(1, PACK):
            nc.sync.dma_start(out=x[t][:], in_=x_rows[:, t, :])
        nc.sync.dma_start(out=fk_sb[:], in_=fk.rearrange("(p t) o -> p (t o)", t=PACK))
        load_scales(w_plane, w_scales)
        load_words(w_codes, w_words)
        load_scales(wb_raw_plane, wb_scales)
        load_words(wb_raw, wb_words)
        nc.sync.dma_start(out=us_sb[:], in_=us.rearrange("o (p t) -> p (o t)", t=PACK))
        nc.sync.dma_start(out=list3[:], in_=offs3)
        for t in range(PACK):
            nc.sync.dma_start(out=table[t][:], in_=tz_rows[:, t, :])

        def part(lst, h):
            return lst[:, h * LIST_COLS : (h + 1) * LIST_COLS]

        second = tiles(sb, "second", HALVES, [P, PACK, S], F32)
        gap = tiles(sb, "gap", HALVES, [P, PACK, S], F32)
        u_planes = tiles(sb, "u_planes", HALVES, [P, PACK - 1, S], BF16)
        u_grouped = tiles(sb, "u_grouped", HALVES, [P, S, PACK], BF16)
        u_codes = tiles(sb, "u_codes", HALVES, [P, S], U32)
        u_scale = tiles(sb, "u_scale", HALVES, [P, S], U8)
        a_ps = banks("a_ps", 2 * HALVES, [P, R_BANK])
        a_sb = tiles(sb, "a_sb", HALVES, [P, PACK, P], F32)
        peak = tiles(sb, "peak", HALVES, [P, R // BUNDLE], F32)
        d_ps = banks("d_ps", HALVES, [P, PACK, S])
        h_codes = tiles(sb, "h_codes", HALVES, [P, S], U32)
        h_scale = tiles(sb, "h_scale", HALVES, [P, S], U8)
        looked = tiles(sb, "looked", HALVES, [P, PACK, S], F32)
        y = tiles(sb, "y", HALVES, [P, PACK, S], F32)
        y_grouped = tiles(sb, "y_grouped", HALVES, [P, S, PACK], BF16)
        y_codes = sb.tile([P, J], U32, name="y_codes", align_bytes=64)
        y_scale = sb.tile([P, J], U8, name="y_scale", align_bytes=64)

        for t in range(PACK):
            for h in range(HALVES):
                nc.scalar.activation(second[h][:, t, :], x[t][:].indirect(part(list2, h)), COPY)
                nc.vector.tensor_tensor(
                    gap[h][:, t, :], x[t][:].indirect(part(list1, h)), second[h][:, t, :], ALU.subtract
                )
        for h in range(HALVES):
            for t in range(PACK - 1):
                nc.scalar.activation(u_planes[h][:, t, :], gap[h][:, t, :], COPY, scale=fk_sb[:, t : t + 1])

        for h in range(HALVES):
            nc.vector.tensor_copy(
                out=u_grouped[h][:, :, 0 : PACK - 1], in_=u_planes[h][:].rearrange("p t j -> p j t")
            )
            nc.vector.tensor_scalar(
                out=u_grouped[h][:, :, PACK - 1],
                in0=gap[h][:, PACK - 1, :],
                scalar1=fk_sb[:, PACK - 1 : PACK],
                scalar2=None,
                op0=ALU.mult,
            )
            quantize(u_codes[h][:], u_scale[h][:], u_grouped[h][:], E5M2)
            for b in range(2):
                cols = slice(b * R_BANK, (b + 1) * R_BANK)
                nc.tensor.matmul_mx(
                    out=a_ps[2 * h + b][:],
                    lhsT=u_codes[h][:].bitcast(E5M2),
                    lhsT_scale=u_scale[h][:],
                    rhs=w_codes[:, cols].bitcast(E5M2),
                    rhs_scale=w_plane[:, cols],
                    start=True,
                    stop=True,
                )

        wb_codes = sb.tile([P, PACK, P], U32, name="wb_codes", tag="u_codes1", align_bytes=64)
        wb_plane = sb.tile([P, PACK, P], U8, name="wb_plane", tag="u_scale1", align_bytes=64)
        nc.gpsimd.tensor_copy(out=wb_codes[:], in_=wb_raw[:].rearrange("p (m t) -> p t m", t=PACK))
        nc.gpsimd.tensor_copy(out=wb_plane[:], in_=wb_raw_plane[:].rearrange("p (m t) -> p t m", t=PACK))

        def peaks(h, b):
            g = R_BANK // BUNDLE
            nc.vector.tensor_reduce(
                out=peak[h][:, b * g : (b + 1) * g],
                in_=a_ps[2 * h + b][:].rearrange("p (g e) -> p g e", e=BUNDLE),
                axis=mybir.AxisListType.X,
                op=ALU.max,
            )

        def above(h, b, ts):
            g = R_BANK // BUNDLE
            q = R_BANK // PACK
            count = ts.stop - ts.start
            nc.vector.scalar_tensor_tensor(
                out=a_sb[h][:, ts, b * q : (b + 1) * q].rearrange("p t q -> p q t"),
                in0=peak[h][:, b * g : (b + 1) * g].unsqueeze(2).to_broadcast([P, g, 2 * count]),
                scalar=-0.5,
                in1=a_ps[2 * h + b][:].rearrange("p (q t) -> p q t", t=PACK)[:, :, ts],
                op0=ALU.mult,
                op1=ALU.add,
            )

        for h in range(HALVES):
            peaks(h, 0)
            peaks(h, 1)
            for ts in [slice(0, PACK)] if h == 0 else [slice(0, 2), slice(2, PACK)]:
                above(h, 0, ts)
                above(h, 1, ts)
                for t in range(ts.start, ts.stop):
                    nc.tensor.transpose(d_ps[h][:, t, :], a_sb[h][:, t, :], ident[:])

        p_ps = []
        for h in range(HALVES):
            h_grouped = sb.tile([P, S, PACK], BF16, name="h_grouped%d" % h, tag="h_grouped", align_bytes=64)
            nc.vector.scalar_tensor_tensor(
                out=h_grouped[:],
                in0=d_ps[h][:].rearrange("p t j -> p j t"),
                scalar=0.0,
                in1=us_sb[:].unsqueeze(1).to_broadcast([P, S, PACK]),
                op0=ALU.max,
                op1=ALU.mult,
            )
            quantize(h_codes[h][:], h_scale[h][:], h_grouped[:], E5M2)
            for u in range(2):
                p_ps.append(ps.tile([P, 2, S], F32, name="p_ps%d" % (2 * h + u), tag="a_ps%d" % (2 * h + u)))
            for t in range(PACK):
                nc.tensor.matmul_mx(
                    out=p_ps[2 * h + t // 2][:, t % 2, :],
                    lhsT=wb_codes[:, t, :].bitcast(E4M3),
                    lhsT_scale=wb_plane[:, t, :],
                    rhs=h_codes[h][:].bitcast(E5M2),
                    rhs_scale=h_scale[h][:],
                    start=True,
                    stop=True,
                )

        y_rows = out_0.rearrange("(p t) j -> p t j", t=PACK)
        words = out_1[0].rearrange("p j t -> p (j t)").bitcast(I32)
        for h in range(HALVES):
            slots = slice(h * S, (h + 1) * S)
            for t in range(PACK):
                nc.scalar.activation(looked[h][:, t, :], table[t][:].indirect(part(list3, h)), COPY)
            for u in range(2):
                rows = slice(2 * u, 2 * u + 2)
                nc.vector.tensor_tensor(y[h][:, rows, :], p_ps[2 * h + u][:], looked[h][:, rows, :], ALU.mult)
            nc.sync.dma_start(out=y_rows[:, :, slots], in_=y[h][:])
            if h == 0:
                nc.scalar.copy(out=y_grouped[h][:], in_=y[h][:].rearrange("p t j -> p j t"))
                quantize(y_codes[:, slots], y_scale[:, slots], y_grouped[h][:], E4M3)
            else:
                quarters = [slice(0, S // 2), slice(S // 2, S)]
                for c in quarters:
                    interleave(nc.vector.tensor_copy, y_grouped[h][:, c, :], y[h][:, :, c])
                for c in quarters:
                    quantize(y_codes[:, slots][:, c], y_scale[:, slots][:, c], y_grouped[h][:, c, :], E4M3)
        nc.sync.dma_start(out=words, in_=y_codes[:].bitcast(I32))
        for q in range(4):
            queue = nc.scalar if q % 2 == 0 else nc.sync
            queue.dma_start(
                out=out_2[0, 4 * q : 4 * q + 4, :].bitcast(I32), in_=y_scale[32 * q : 32 * q + 4, :].bitcast(I32)
            )
